import numpy as np
import ml_dtypes


def mxq(x, axis, fmt="e4m3"):
    dtype, down = {"e4m3": (ml_dtypes.float8_e4m3fn, 7), "e5m2": (ml_dtypes.float8_e5m2, 14)}[fmt]
    v = np.moveaxis(np.asarray(x, np.float32).astype(ml_dtypes.bfloat16).astype(np.float64), axis, -1)
    blocks = v.reshape(v.shape[:-1] + (-1, 32))
    amax = np.abs(blocks).max(-1, keepdims=True)
    byte = np.maximum(np.where(amax > 0, np.frexp(amax)[1] - 1 + 127, 0) - down, 1)
    scale = np.exp2(byte - 127.0)
    codes = (blocks / scale).astype(np.float32).astype(dtype).astype(np.float64)
    return np.moveaxis((codes * scale).reshape(v.shape), -1, axis)


WIDE = False


def mx_kscale(k):
    if not WIDE:
        return np.ones(k)
    levels = np.array([10, -10, 5, -5, 0])
    if k % 512:
        return np.exp2(np.random.permutation(np.resize(levels, k // 32))).repeat(32)
    a = np.empty((k // 512, 16))
    for p in range(k // 512):
        a[p, :8] = np.random.permutation(np.resize(levels, 8))
        for g in range(8):
            far = levels[np.abs(levels - a[p, g]) >= 10]
            a[p, g + 8] = far[np.random.randint(len(far))]
    return np.exp2(a.ravel()).repeat(32)


def f64(x):
    return np.asarray(x).astype(np.float64)


def striped(idx):
    return np.tile(idx.reshape(-1, 16).T, (8, 1)).astype(np.uint16)


def unstriped(offs):
    return offs[:16].T.reshape(-1).astype(np.int64)


E2M1 = np.array([0.0, 0.5, 1.0, 1.5, 2.0, 3.0, 4.0, 6.0, -0.0, -0.5, -1.0, -1.5, -2.0, -3.0, -4.0, -6.0])


def pack_weight(w, fmt):
    k, n = w.shape
    w = f64(np.asarray(w, np.float32).astype(ml_dtypes.bfloat16)).reshape(k // 32, 32, n)
    amax = np.abs(w).max(1)
    if fmt == "e4m3":
        byte = np.frexp(amax)[1] - 1 + 127 - 7
    else:
        mant, ex = np.frexp(amax / 6.0)
        byte = np.where(mant > 0.5, ex, ex - 1) + 127
    byte = np.clip(np.where(amax > 0, byte, 1), 1, 254)
    scaled = (w * np.exp2(127.0 - byte)[:, None, :]).reshape(k, n).astype(np.float32)
    by_word = np.ascontiguousarray(scaled.reshape(k // 512, 128, 4, n).transpose(0, 1, 3, 2))
    if fmt == "e4m3":
        words = by_word.astype(ml_dtypes.float8_e4m3fn).view(np.uint8)
    else:
        c = by_word.astype(ml_dtypes.float4_e2m1fn).view(np.uint8) & 0xF
        words = (c[..., 0::2] | (c[..., 1::2] << 4)).reshape(k // 512, 128, 2 * n)
    return np.ascontiguousarray(words), np.ascontiguousarray(byte.astype(np.uint8).reshape(k // 512, 16, n))


def unpack_weight(words, scales, fmt):
    g, _, n = scales.shape
    words = np.ascontiguousarray(words).reshape(g, 128, n, -1)
    if fmt == "e4m3":
        vals = words.view(ml_dtypes.float8_e4m3fn).astype(np.float64)
    else:
        nib = np.empty((g, 128, n, 4), np.uint8)
        nib[..., 0::2] = words & 0xF
        nib[..., 1::2] = words >> 4
        vals = E2M1[nib]
    vals = vals * np.repeat(np.exp2(scales.astype(np.float64) - 127.0), 8, axis=1)[..., None]
    return vals.transpose(0, 1, 3, 2).reshape(g * 512, n)


def gelu(v):
    return 0.5 * v * (1.0 + np.tanh(np.sqrt(2.0 / np.pi) * (v + 0.044715 * v**3)))


K, H, N, T, S, P, T2 = 1024, 512, 384, 4096, 1024, 1024, 2048

def setup_inputs():
    n = np.random.standard_normal
    s = mx_kscale(K)[:, None]
    u = mx_kscale(H)[:, None]
    d = {}
    d["tab_words"], d["tab_scales"] = pack_weight(n((K, T)) * s, "e4m3")
    d["offs"] = striped(np.random.permutation(T)[:S])
    d["offs2"] = striped(np.random.permutation(T2)[:S])
    d["offs3"] = striped(np.random.permutation(T2)[:P])
    d["offs4"] = striped(np.random.permutation(T2)[:P])
    d["w1"] = (1.6 * n((K, H)) / K**0.5 / s).astype(np.float32)
    d["w2_words"], d["w2_scales"] = pack_weight(1.5 * n((K, H)) / K**0.5 / s, "e2m1")
    d["gain"] = (np.random.uniform(0.4, 0.8, H) * u[:, 0]).astype(np.float32)
    d["page0"] = (n((H, T2)) * u).astype(np.float32)
    d["wgs"] = np.exp(0.3 * n((128, S))).astype(np.float32)
    d["shift"] = (0.6 * n(H) * u[:, 0]).astype(np.float32)
    d["w3"] = (0.9 * n((H, N)) / H**0.5 / u).astype(np.float32)
    d["base"] = n(N).astype(np.float32)
    d["page1"] = (1.5 * n((N, T2))).astype(np.float32)
    d["wgo"] = np.exp(0.3 * n((128, P))).astype(np.float32)
    return d

def reference(tab_words, tab_scales, offs, offs2, offs3, offs4, w1, w2_words, w2_scales, gain, page0, wgs, shift, w3, base, page1, wgo):
    v = unpack_weight(tab_words, tab_scales, "e4m3")[:, unstriped(offs)]
    a = mxq(f64(w1), 0, "e4m3").T @ v
    b = unpack_weight(w2_words, w2_scales, "e2m1").T @ v
    h = f64(gain)[:, None] * (a + np.tanh(a) * b)
    page = f64(page0).copy()
    page[:, unstriped(offs2)] = np.tile(f64(wgs), (H // 128, 1)) * h
    x = page[:, unstriped(offs3)] + f64(shift)[:, None]
    e = mxq(f64(w3), 0, "e4m3").T @ mxq(x, 0, "e4m3")
    y = np.square(e) + f64(base)[:, None]
    out = f64(page1).copy()
    out[:, unstriped(offs4)] = np.tile(f64(wgo), (N // 128, 1)) * y
    return out

@@ -1,0 +1,326 @@
+from contextlib import ExitStack
+
+import concourse.mybir as mybir
+
+K, H, N, T, S, PICKS, T2 = 1024, 512, 384, 4096, 1024, 1024, 2048
+
+F32 = mybir.dt.float32
+BF16 = mybir.dt.bfloat16
+I32 = mybir.dt.int32
+U32 = mybir.dt.uint32
+U16 = mybir.dt.uint16
+U8 = mybir.dt.uint8
+FP8X4 = mybir.dt.float8_e4m3fn_x4
+FP4X4 = mybir.dt.float4_e2m1fn_x4
+ACT = mybir.ActivationFunctionType
+ALU = mybir.AluOpType
+
+P = 128
+PACK = 4
+PASSES = K // (P * PACK)
+HALF = 512
+PER_COL = 16
+N_TILES = N // P
+CHUNKS = ((0, 256), (256, 512), (512, 1024))
+
+FLOPS = 2 * K * H * S * 2 + 2 * H * N * PICKS
+
+
+def tile_list_larval_ration_page_kernel(
+    tc, tab_words, tab_scales, offs, offs2, offs3, offs4, w1, w2_words, w2_scales,
+    gain, page0, wgs, shift, w3, base, page1, wgo, out,
+):
+    nc = tc.nc
+
+    def entries(offsets, lo, hi):
+        return offsets[:, lo // PER_COL : hi // PER_COL]
+
+    with ExitStack() as ctx:
+        lists = ctx.enter_context(tc.tile_pool(name="lists", bufs=1))
+        keep = ctx.enter_context(tc.tile_pool(name="keep", bufs=1))
+        ring = ctx.enter_context(tc.tile_pool(name="ring", bufs=2))
+        psum = ctx.enter_context(tc.psum_pool(name="psum", bufs=2))
+
+        list1 = lists.tile([P, S // PER_COL], U16, name="list1")
+        list2 = lists.tile([P, S // PER_COL], U16, name="list2")
+        list3 = lists.tile([P, PICKS // PER_COL], U16, name="list3")
+        list4 = lists.tile([P, PICKS // PER_COL], U16, name="list4")
+
+        warm = keep.tile([P, 2], F32, name="warm")
+        nc.gpsimd.memset(warm[:, 0:1], 0.0)
+        warmed = keep.tile([P, 2], F32, name="warmed")
+        nc.scalar.activation(warmed[:, 0:1], warm[:, 0:1], ACT.Tanh)
+        nc.sync.dma_start(list1[:], offs)
+        tab_sc = keep.tile([P, T], U8, name="tab_sc", tag="tab_sc", align_bytes=64)
+        nc.sync.dma_start(
+            tab_sc[0:32, :].bitcast(I32), tab_scales.rearrange("a q t -> q a t").bitcast(I32)
+        )
+        nc.vector.memset(tab_sc[32:64, :].bitcast(I32), 0)
+        nc.vector.memset(tab_sc[64:128, :].bitcast(I32), 0)
+
+        tab = [
+            keep.tile([P, T], I32, name="tab%d" % a, tag="tab%d" % a, align_bytes=64) for a in range(PASSES)
+        ]
+        w1_raw = [
+            keep.tile([P, PACK, H], F32, name="w1_raw%d" % a, tag="w1_raw%d" % a, align_bytes=64)
+            for a in range(PASSES)
+        ]
+        w2_raw = keep.tile([P, PASSES, 2 * H], U8, name="w2_raw")
+
+        def load_tab(a):
+            nc.sync.dma_start(tab[a][:], tab_words[a].rearrange("p t i -> p (t i)").bitcast(I32))
+
+        w2s_raw = keep.tile([P, H], U8, name="w2s_raw")
+        nc.sync.dma_start(
+            w2s_raw[0:32, :].bitcast(I32), w2_scales.rearrange("a q c -> q a c").bitcast(I32)
+        )
+        nc.gpsimd.memset(w2s_raw[32:64, :].bitcast(I32), 0)
+        nc.gpsimd.memset(w2s_raw[64:128, :].bitcast(I32), 0)
+        for a in range(PASSES):
+            nc.sync.dma_start(
+                w1_raw[a][:], w1[a * 512 : (a + 1) * 512, :].rearrange("(p j) c -> p j c", j=PACK)
+            )
+        load_tab(0)
+        nc.sync.dma_start(w2_raw[:].bitcast(I32), w2_words.rearrange("a p c -> p a c").bitcast(I32))
+        load_tab(1)
+        gain_sb = keep.tile([P, PACK], F32, name="gain_sb")
+        shift_sb = keep.tile([P, PACK], F32, name="shift_sb")
+        base_sb = keep.tile([P, N_TILES], F32, name="base_sb")
+        nc.sync.dma_start(gain_sb[:], gain.rearrange("(p t) -> p t", t=PACK))
+        nc.sync.dma_start(list2[:], offs2)
+
+        picked_sc = keep.tile([P, S], U8, name="picked_sc")
+        nc.vector.tensor_copy(picked_sc[:], tab_sc[:].indirect(list1[:]))
+        compact = keep.tile([P, S + H], U8, name="compact")
+        nc.vector.tensor_copy(
+            compact[:, S:].rearrange("p (t q) -> p q t", t=PACK),
+            w2s_raw[:].rearrange("p (q t) -> p q t", t=PACK),
+        )
+        nc.vector.tensor_copy(compact[:, :S].bitcast(I32), picked_sc[:].bitcast(I32))
+        planes = keep.tile([P, PASSES, S + H], U8, name="planes", align_bytes=64)
+        nc.gpsimd.memset(planes[:].bitcast(I32), 0)
+        for q in range(4):
+            nc.scalar.dma_start(
+                planes[32 * q : 32 * q + 4, :, :].bitcast(I32),
+                compact[8 * q : 8 * q + 8, :].bitcast(I32),
+            )
+
+        wgs_rows = wgs.rearrange("(q t) j -> t q j", t=PACK)
+        page_rows = page0.rearrange("(p t) c -> t p c", t=PACK)
+        wgs_sb = {}
+        page = []
+        for t in range(PACK):
+            spans = ((0, HALF), (HALF, S)) if t == 0 else ((0, S),)
+            page_t = keep.tile([P, T2], F32, name="page%d" % t)
+            page.append(page_t)
+            nc.sync.dma_start(page_t[:], page_rows[t])
+            for lo, hi in spans:
+                dealt = keep.tile(
+                    [P, hi - lo], F32, name="wgs%d_%d" % (t, lo), tag="wgs%d_%d" % (t, lo), align_bytes=64
+                )
+                for q in (0, 2, 1, 3):
+                    nc.sync.dma_start(dealt[32 * q : 32 * q + 32, :], wgs_rows[t][:, lo:hi])
+                for h0 in range(lo, hi, HALF):
+                    wgs_sb[(t, h0)] = dealt[:, h0 - lo : h0 - lo + HALF]
+            if t == 0:
+                nc.sync.dma_start(list3[:], offs3)
+                nc.sync.dma_start(shift_sb[:], shift.rearrange("(p t) -> p t", t=PACK))
+        w3_raw = keep.tile([P, PACK, N], F32, name="w3_raw")
+        nc.sync.dma_start(w3_raw[:], w3.rearrange("(p j) n -> p j n", j=PACK))
+        wgo_sb = keep.tile([P, PICKS], F32, name="wgo_sb")
+        nc.sync.dma_start(wgo_sb[:], wgo)
+        nc.sync.dma_start(list4[:], offs4)
+        with nc.allow_non_contiguous_dma(reason="one bias value a partition"):
+            nc.sync.dma_start(base_sb[:], base.rearrange("(c p) -> p c", p=P))
+
+        v_words = {}
+
+        def pick_words(a):
+            for h0 in range(0, S, HALF):
+                words = keep.tile([P, HALF], U32, name="v_words%d_%d" % (a, h0), align_bytes=64)
+                nc.vector.tensor_copy(
+                    words[:], tab[a][:].bitcast(U32).indirect(entries(list1, h0, h0 + HALF))
+                )
+                v_words[(a, h0)] = words
+
+        w1_codes, w1_scales = [], []
+        for a in range(PASSES):
+            grouped = keep.tile([P, PACK, P, PACK], BF16, name="w1_grouped%d" % a, align_bytes=64)
+            nc.scalar.copy(
+                grouped[:].rearrange("p t q j -> p q t j"),
+                w1_raw[a][:].rearrange("p j (q t) -> p q t j", t=PACK),
+            )
+            codes = keep.tile([P, H], U32, name="w1_codes%d" % a, align_bytes=64)
+            scales = keep.tile([P, H], U8, name="w1_scales%d" % a, align_bytes=64)
+            nc.vector.quantize_mx(
+                out=codes[:].bitcast(FP8X4),
+                scales=scales[:],
+                in_=grouped[:].rearrange("p t q j -> p (t q j)"),
+            )
+            w1_codes.append(codes)
+            w1_scales.append(scales)
+
+        pick_words(0)
+
+        w2_codes = keep.tile([P, PASSES, 2 * H], U8, name="w2_codes", tag="tab0", align_bytes=64)
+        nc.vector.tensor_copy(
+            w2_codes[:].bitcast(U16).rearrange("p a (t q) -> p a q t", t=PACK),
+            w2_raw[:].bitcast(U16).rearrange("p a (q t) -> p a q t", t=PACK),
+        )
+
+        pick_words(1)
+
+        x_rows = [
+            keep.tile([P, PACK, hi - lo], BF16, name="x_rows%d" % c) for c, (lo, hi) in enumerate(CHUNKS)
+        ]
+
+        def fetch(t, lo, hi, dst):
+            nc.vector.tensor_copy(dst, page[t][:].indirect(entries(list3, lo, hi)))
+            for c, (c_lo, c_hi) in enumerate(CHUNKS):
+                if lo <= c_lo and c_hi <= hi:
+                    nc.scalar.activation(
+                        x_rows[c][:, t, :], dst[:, c_lo - lo : c_hi - lo], ACT.Identity,
+                        bias=shift_sb[:, t : t + 1],
+                    )
+
+        steps = [(t, h0) for t in range(PACK) for h0 in range(0, S, HALF)]
+        sums_a, gated_b, states = {}, {}, {}
+
+        def first_products(k):
+            t, h0 = steps[k]
+            cols = slice(t * P, (t + 1) * P)
+            acc_a = psum.tile([P, HALF], F32, name="acc_a", bufs=3)
+            acc_b = psum.tile([P, HALF], F32, name="acc_b", bufs=3)
+            for a in range(PASSES):
+                moving = dict(
+                    rhs=v_words[(a, h0)][:].bitcast(FP8X4),
+                    rhs_scale=planes[:, a, h0 : h0 + HALF],
+                    start=(a == 0),
+                    stop=(a == PASSES - 1),
+                )
+                nc.tensor.matmul_mx(
+                    out=acc_a[:], lhsT=w1_codes[a][:, cols].bitcast(FP8X4),
+                    lhsT_scale=w1_scales[a][:, cols], **moving,
+                )
+                nc.tensor.matmul_mx(
+                    out=acc_b[:], lhsT=w2_codes[:, a, 2 * t * P : 2 * (t + 1) * P].bitcast(FP4X4),
+                    lhsT_scale=planes[:, a, S + t * P : S + (t + 1) * P], **moving,
+                )
+            tanh_a = ring.tile([P, HALF], F32, name="tanh_a", bufs=3)
+            nc.scalar.activation(tanh_a[:], acc_a[:], ACT.Tanh)
+            gated = ring.tile([P, HALF], F32, name="gated")
+            nc.vector.scalar_tensor_tensor(
+                gated[:], acc_b[:], gain_sb[:, t : t + 1], tanh_a[:], ALU.mult, ALU.mult
+            )
+            sums_a[k], gated_b[k] = acc_a, gated
+
+        def new_state(k):
+            t = steps[k][0]
+            state = ring.tile([P, HALF], F32, name="state")
+            nc.vector.scalar_tensor_tensor(
+                state[:], sums_a[k][:], gain_sb[:, t : t + 1], gated_b[k][:], ALU.mult, ALU.add
+            )
+            states[k] = state
+
+        def put_state(k):
+            t, h0 = steps[k]
+            nc.vector.tensor_tensor(
+                page[t][:].indirect(entries(list2, h0, h0 + HALF)), states[k][:], wgs_sb[(t, h0)], ALU.mult
+            )
+
+        first_products(0)
+        for k, (t, h0) in enumerate(steps):
+            new_state(k)
+            if h0 == 0 and t > 0:
+                early = ring.tile([P, HALF], F32, name="early")
+                fetch(t - 1, 0, HALF, early[:])
+            if k + 1 < len(steps):
+                first_products(k + 1)
+            put_state(k)
+
+        ration = []
+        for n, tag in enumerate(("w1_raw0", "w1_raw1", "tab1")):
+            tile_n = keep.tile([P, T2], F32, name="ration%d" % n, tag=tag, align_bytes=64)
+            nc.sync.dma_start(tile_n[:], page1[n * P : (n + 1) * P, :])
+            ration.append(tile_n)
+
+        w3_grouped = keep.tile([P, N, PACK], BF16, name="w3_grouped", tag="wgs1_0", align_bytes=64)
+        nc.scalar.copy(
+            w3_grouped[:].rearrange("p (c i) j -> p c j i", i=4),
+            w3_raw[:].rearrange("p j (c i) -> p c j i", i=4),
+        )
+        w3_codes = keep.tile([P, N], U32, name="w3_codes", align_bytes=64)
+        w3_scales = keep.tile([P, N], U8, name="w3_scales", align_bytes=64)
+        for lo, hi in ((0, 256), (256, 384)):
+            nc.vector.quantize_mx(
+                out=w3_codes[:, lo:hi].bitcast(FP8X4),
+                scales=w3_scales[:, lo:hi],
+                in_=w3_grouped[:, lo:hi, :].rearrange("p n j -> p (n j)"),
+            )
+
+        x_grouped = {}
+
+        def weave(c):
+            lo, hi = CHUNKS[c]
+            grouped = keep.tile(
+                [P, hi - lo, PACK], BF16, name="x_grouped%d" % c, tag="x_grouped%d" % c, align_bytes=64
+            )
+            nc.scalar.copy(
+                grouped[:].rearrange("p (m i) t -> p m t i", i=4),
+                x_rows[c][:].rearrange("p t (m i) -> p m t i", i=4),
+            )
+            x_grouped[c] = grouped
+
+        features = {}
+
+        def second_product(c):
+            lo, hi = CHUNKS[c]
+            codes = keep.tile([P, hi - lo], U32, name="x_codes%d" % c, align_bytes=64)
+            scales = keep.tile([P, hi - lo], U8, name="x_scales%d" % c, align_bytes=64)
+            nc.vector.quantize_mx(
+                out=codes[:].bitcast(FP8X4), scales=scales[:],
+                in_=x_grouped[c][:].rearrange("p m t -> p (m t)"),
+            )
+            for n in range(N_TILES):
+                acc_e = psum.tile([P, HALF], F32, name="acc_e")
+                nc.tensor.matmul_mx(
+                    out=acc_e[:, : hi - lo],
+                    lhsT=w3_codes[:, n * P : (n + 1) * P].bitcast(FP8X4),
+                    lhsT_scale=w3_scales[:, n * P : (n + 1) * P],
+                    rhs=codes[:].bitcast(FP8X4), rhs_scale=scales[:], start=True, stop=True,
+                )
+                squared = ring.tile([P, hi - lo], F32, name="squared")
+                nc.scalar.activation(squared[:], acc_e[:, : hi - lo], ACT.Square)
+                feature = keep.tile([P, hi - lo], F32, name="feature%d_%d" % (c, n))
+                nc.scalar.activation(feature[:], squared[:], ACT.Identity, bias=base_sb[:, n : n + 1])
+                features[(c, n)] = feature
+
+        def place(c, n):
+            lo, hi = CHUNKS[c]
+            nc.vector.tensor_tensor(
+                ration[n][:].indirect(entries(list4, lo, hi)), features[(c, n)][:], wgo_sb[:, lo:hi], ALU.mult
+            )
+
+        for c in (0, 1):
+            lo, hi = CHUNKS[c]
+            last = ring.tile([P, hi - lo], F32, name="last")
+            fetch(PACK - 1, lo, hi, last[:])
+            weave(c)
+        lo, hi = CHUNKS[2]
+        for t in (0, 1):
+            early = ring.tile([P, HALF], F32, name="early")
+            fetch(t, lo, hi, early[:])
+        second_product(0)
+        late = keep.tile([P, 2, HALF], F32, name="late", tag="x_grouped0", align_bytes=64)
+        for t in (2, 3):
+            fetch(t, lo, hi, late[:, t - 2, :])
+        second_product(1)
+        weave(2)
+        for n in range(N_TILES):
+            place(0, n)
+        second_product(2)
+        for n in range(N_TILES):
+            place(1, n)
+        for n in range(N_TILES):
+            place(2, n)
+            nc.sync.dma_start(out[n * P : (n + 1) * P, :], ration[n][:])

@@ -1,6 +1,7 @@
 from contextlib import ExitStack
 
 import concourse.mybir as mybir
+from concourse.masks import make_identity
 
 K, H, N, T, S, PICKS, T2 = 1024, 512, 384, 4096, 1024, 1024, 2048
 
@@ -21,6 +22,7 @@ PASSES = K // (P * PACK)
 HALF = 512
 PER_COL = 16
 N_TILES = N // P
+DIRECT = 1
 CHUNKS = ((0, 256), (256, 512), (512, 1024))
 
 FLOPS = 2 * K * H * S * 2 + 2 * H * N * PICKS
@@ -55,7 +57,7 @@ def tile_list_larval_ration_page_kernel(
         nc.sync.dma_start(
             tab_sc[0:32, :].bitcast(I32), tab_scales.rearrange("a q t -> q a t").bitcast(I32)
         )
-        nc.vector.memset(tab_sc[32:64, :].bitcast(I32), 0)
+        nc.gpsimd.memset(tab_sc[32:64, :].bitcast(I32), 0)
         nc.vector.memset(tab_sc[64:128, :].bitcast(I32), 0)
 
         tab = [
@@ -76,18 +78,23 @@ def tile_list_larval_ration_page_kernel(
         )
         nc.gpsimd.memset(w2s_raw[32:64, :].bitcast(I32), 0)
         nc.gpsimd.memset(w2s_raw[64:128, :].bitcast(I32), 0)
-        for a in range(PASSES):
+        def load_w1(a):
             nc.sync.dma_start(
                 w1_raw[a][:], w1[a * 512 : (a + 1) * 512, :].rearrange("(p j) c -> p j c", j=PACK)
             )
-        load_tab(0)
-        nc.sync.dma_start(w2_raw[:].bitcast(I32), w2_words.rearrange("a p c -> p a c").bitcast(I32))
-        load_tab(1)
+
         gain_sb = keep.tile([P, PACK], F32, name="gain_sb")
         shift_sb = keep.tile([P, PACK], F32, name="shift_sb")
         base_sb = keep.tile([P, N_TILES], F32, name="base_sb")
+        load_w1(0)
         nc.sync.dma_start(gain_sb[:], gain.rearrange("(p t) -> p t", t=PACK))
         nc.sync.dma_start(list2[:], offs2)
+        nc.sync.dma_start(list3[:], offs3)
+        nc.sync.dma_start(list4[:], offs4)
+        load_w1(1)
+        load_tab(0)
+        nc.sync.dma_start(w2_raw[:].bitcast(I32), w2_words.rearrange("a p c -> p a c").bitcast(I32))
+        nc.sync.dma_start(shift_sb[:], shift.rearrange("(p t) -> p t", t=PACK))
 
         picked_sc = keep.tile([P, S], U8, name="picked_sc")
         nc.vector.tensor_copy(picked_sc[:], tab_sc[:].indirect(list1[:]))
@@ -100,10 +107,11 @@ def tile_list_larval_ration_page_kernel(
         planes = keep.tile([P, PASSES, S + H], U8, name="planes", align_bytes=64)
         nc.gpsimd.memset(planes[:].bitcast(I32), 0)
         for q in range(4):
-            nc.scalar.dma_start(
+            nc.sync.dma_start(
                 planes[32 * q : 32 * q + 4, :, :].bitcast(I32),
                 compact[8 * q : 8 * q + 8, :].bitcast(I32),
             )
+        load_tab(1)
 
         wgs_rows = wgs.rearrange("(q t) j -> t q j", t=PACK)
         page_rows = page0.rearrange("(p t) c -> t p c", t=PACK)
@@ -122,14 +130,10 @@ def tile_list_larval_ration_page_kernel(
                     nc.sync.dma_start(dealt[32 * q : 32 * q + 32, :], wgs_rows[t][:, lo:hi])
                 for h0 in range(lo, hi, HALF):
                     wgs_sb[(t, h0)] = dealt[:, h0 - lo : h0 - lo + HALF]
-            if t == 0:
-                nc.sync.dma_start(list3[:], offs3)
-                nc.sync.dma_start(shift_sb[:], shift.rearrange("(p t) -> p t", t=PACK))
         w3_raw = keep.tile([P, PACK, N], F32, name="w3_raw")
         nc.sync.dma_start(w3_raw[:], w3.rearrange("(p j) n -> p j n", j=PACK))
         wgo_sb = keep.tile([P, PICKS], F32, name="wgo_sb")
         nc.sync.dma_start(wgo_sb[:], wgo)
-        nc.sync.dma_start(list4[:], offs4)
         with nc.allow_non_contiguous_dma(reason="one bias value a partition"):
             nc.sync.dma_start(base_sb[:], base.rearrange("(c p) -> p c", p=P))
 
@@ -186,40 +190,70 @@ def tile_list_larval_ration_page_kernel(
         steps = [(t, h0) for t in range(PACK) for h0 in range(0, S, HALF)]
         sums_a, gated_b, states = {}, {}, {}
 
+        identity = keep.tile([P, P], F32, name="identity")
+        make_identity(nc, identity[:])
+
+        def operands(a, t, lo, hi):
+            h0 = lo // HALF * HALF
+            table = (v_words[(a, h0)][:, lo - h0 : hi - h0].bitcast(FP8X4), planes[:, a, lo:hi])
+            first = (w1_codes[a][:, t * P : (t + 1) * P].bitcast(FP8X4), w1_scales[a][:, t * P : (t + 1) * P])
+            second = (
+                w2_codes[:, a, 2 * t * P : 2 * (t + 1) * P].bitcast(FP4X4),
+                planes[:, a, S + t * P : S + (t + 1) * P],
+            )
+            return table, first, second
+
+        def mx_pass(acc, stationary, moving, a):
+            nc.tensor.matmul_mx(
+                out=acc, lhsT=stationary[0], lhsT_scale=stationary[1], rhs=moving[0], rhs_scale=moving[1],
+                start=(a == 0), stop=(a == PASSES - 1),
+            )
+
         def first_products(k):
             t, h0 = steps[k]
-            cols = slice(t * P, (t + 1) * P)
-            acc_a = psum.tile([P, HALF], F32, name="acc_a", bufs=3)
-            acc_b = psum.tile([P, HALF], F32, name="acc_b", bufs=3)
-            for a in range(PASSES):
-                moving = dict(
-                    rhs=v_words[(a, h0)][:].bitcast(FP8X4),
-                    rhs_scale=planes[:, a, h0 : h0 + HALF],
-                    start=(a == 0),
-                    stop=(a == PASSES - 1),
-                )
-                nc.tensor.matmul_mx(
-                    out=acc_a[:], lhsT=w1_codes[a][:, cols].bitcast(FP8X4),
-                    lhsT_scale=w1_scales[a][:, cols], **moving,
-                )
-                nc.tensor.matmul_mx(
-                    out=acc_b[:], lhsT=w2_codes[:, a, 2 * t * P : 2 * (t + 1) * P].bitcast(FP4X4),
-                    lhsT_scale=planes[:, a, S + t * P : S + (t + 1) * P], **moving,
-                )
+            acc_a = psum.tile([P, HALF], F32, name="acc_a")
+            acc_b = psum.tile([P, HALF], F32, name="acc_b")
             tanh_a = ring.tile([P, HALF], F32, name="tanh_a", bufs=3)
+            if k < DIRECT:
+                for a in range(PASSES):
+                    table, first, second = operands(a, t, h0, h0 + HALF)
+                    mx_pass(acc_a[:], first, table, a)
+                    mx_pass(acc_b[:], second, table, a)
+                nc.scalar.activation(tanh_a[:], acc_a[:], ACT.Tanh)
+                gated = keep.tile([P, HALF], F32, name="gated_direct", tag="state-1", align_bytes=64)
+                nc.vector.scalar_tensor_tensor(
+                    gated[:], acc_b[:], gain_sb[:, t : t + 1], tanh_a[:], ALU.mult, ALU.mult
+                )
+                sums_a[k], gated_b[k] = acc_a, gated
+                return
+            for which, acc in ((1, acc_a), (2, acc_b)):
+                for lo in range(0, HALF, P):
+                    for a in range(PASSES):
+                        three = operands(a, t, h0 + lo, h0 + lo + P)
+                        mx_pass(acc[:, lo : lo + P], three[0], three[which], a)
             nc.scalar.activation(tanh_a[:], acc_a[:], ACT.Tanh)
-            gated = ring.tile([P, HALF], F32, name="gated")
-            nc.vector.scalar_tensor_tensor(
-                gated[:], acc_b[:], gain_sb[:, t : t + 1], tanh_a[:], ALU.mult, ALU.mult
-            )
-            sums_a[k], gated_b[k] = acc_a, gated
+            plain = ring.tile([P, HALF], F32, name="plain", bufs=3)
+            nc.scalar.copy(plain[:], acc_a[:])
+            gated = keep.tile([P, HALF], F32, name="gated%d" % k, tag="state%d" % (k - 2), align_bytes=64)
+            nc.vector.tensor_tensor(gated[:], acc_b[:], tanh_a[:], ALU.mult)
+            sums_a[k], gated_b[k] = plain, gated
 
         def new_state(k):
             t = steps[k][0]
-            state = ring.tile([P, HALF], F32, name="state")
-            nc.vector.scalar_tensor_tensor(
-                state[:], sums_a[k][:], gain_sb[:, t : t + 1], gated_b[k][:], ALU.mult, ALU.add
-            )
+            state = keep.tile([P, HALF], F32, name="state%d" % k, tag="state%d" % k, align_bytes=64)
+            if k < DIRECT:
+                nc.vector.scalar_tensor_tensor(
+                    state[:], sums_a[k][:], gain_sb[:, t : t + 1], gated_b[k][:], ALU.mult, ALU.add
+                )
+            else:
+                summed = psum.tile([P, HALF], F32, name="summed")
+                for lo in range(0, HALF, P):
+                    for term, addend in enumerate((sums_a[k], gated_b[k])):
+                        nc.tensor.matmul(
+                            summed[:, lo : lo + P], addend[:, lo : lo + P], identity[:],
+                            start=(term == 0), stop=(term == 1), is_transpose=True,
+                        )
+                nc.scalar.activation(state[:], summed[:], ACT.Copy, scale=gain_sb[:, t : t + 1])
             states[k] = state
 
         def put_state(k):
@@ -230,12 +264,15 @@ def tile_list_larval_ration_page_kernel(
 
         first_products(0)
         for k, (t, h0) in enumerate(steps):
-            new_state(k)
-            if h0 == 0 and t > 0:
-                early = ring.tile([P, HALF], F32, name="early")
-                fetch(t - 1, 0, HALF, early[:])
+            if k < DIRECT:
+                new_state(k)
             if k + 1 < len(steps):
                 first_products(k + 1)
+            if k >= DIRECT:
+                new_state(k)
+            if h0 == HALF and t > 0:
+                early = ring.tile([P, HALF], F32, name="early")
+                fetch(t - 1, 0, HALF, early[:])
             put_state(k)
 
         ration = []
@@ -307,9 +344,9 @@ def tile_list_larval_ration_page_kernel(
             fetch(PACK - 1, lo, hi, last[:])
             weave(c)
         lo, hi = CHUNKS[2]
-        for t in (0, 1):
-            early = ring.tile([P, HALF], F32, name="early")
-            fetch(t, lo, hi, early[:])
+        for t, tag in ((0, "state7"), (1, "wgs3_0")):
+            held = keep.tile([P, HALF], F32, name="held%d" % t, tag=tag, align_bytes=64)
+            fetch(t, lo, hi, held[:])
         second_product(0)
         late = keep.tile([P, 2, HALF], F32, name="late", tag="x_grouped0", align_bytes=64)
         for t in (2, 3):

@@ -22,7 +22,7 @@ PASSES = K // (P * PACK)
 HALF = 512
 PER_COL = 16
 N_TILES = N // P
-DIRECT = 1
+DIRECT = 2
 CHUNKS = ((0, 256), (256, 512), (512, 1024))
 
 FLOPS = 2 * K * H * S * 2 + 2 * H * N * PICKS
@@ -48,10 +48,6 @@ def tile_list_larval_ration_page_kernel(
         list3 = lists.tile([P, PICKS // PER_COL], U16, name="list3")
         list4 = lists.tile([P, PICKS // PER_COL], U16, name="list4")
 
-        warm = keep.tile([P, 2], F32, name="warm")
-        nc.gpsimd.memset(warm[:, 0:1], 0.0)
-        warmed = keep.tile([P, 2], F32, name="warmed")
-        nc.scalar.activation(warmed[:, 0:1], warm[:, 0:1], ACT.Tanh)
         nc.sync.dma_start(list1[:], offs)
         tab_sc = keep.tile([P, T], U8, name="tab_sc", tag="tab_sc", align_bytes=64)
         nc.sync.dma_start(
@@ -220,7 +216,7 @@ def tile_list_larval_ration_page_kernel(
                     mx_pass(acc_a[:], first, table, a)
                     mx_pass(acc_b[:], second, table, a)
                 nc.scalar.activation(tanh_a[:], acc_a[:], ACT.Tanh)
-                gated = keep.tile([P, HALF], F32, name="gated_direct", tag="state-1", align_bytes=64)
+                gated = keep.tile([P, HALF], F32, name="gated_direct")
                 nc.vector.scalar_tensor_tensor(
                     gated[:], acc_b[:], gain_sb[:, t : t + 1], tanh_a[:], ALU.mult, ALU.mult
                 )

@@ -22,7 +22,7 @@ PASSES = K // (P * PACK)
 HALF = 512
 PER_COL = 16
 N_TILES = N // P
-DIRECT = 2
+DIRECT = 1
 CHUNKS = ((0, 256), (256, 512), (512, 1024))
 
 FLOPS = 2 * K * H * S * 2 + 2 * H * N * PICKS
@@ -65,8 +65,10 @@ def tile_list_larval_ration_page_kernel(
         ]
         w2_raw = keep.tile([P, PASSES, 2 * H], U8, name="w2_raw")
 
-        def load_tab(a):
-            nc.sync.dma_start(tab[a][:], tab_words[a].rearrange("p t i -> p (t i)").bitcast(I32))
+        def load_tab(a, pieces):
+            words = tab_words[a].rearrange("p t i -> p (t i)").bitcast(I32)
+            for lo in range(0, T, T // pieces):
+                nc.sync.dma_start(tab[a][:, lo : lo + T // pieces], words[:, lo : lo + T // pieces])
 
         w2s_raw = keep.tile([P, H], U8, name="w2s_raw")
         nc.sync.dma_start(
@@ -74,23 +76,19 @@ def tile_list_larval_ration_page_kernel(
         )
         nc.gpsimd.memset(w2s_raw[32:64, :].bitcast(I32), 0)
         nc.gpsimd.memset(w2s_raw[64:128, :].bitcast(I32), 0)
-        def load_w1(a):
-            nc.sync.dma_start(
-                w1_raw[a][:], w1[a * 512 : (a + 1) * 512, :].rearrange("(p j) c -> p j c", j=PACK)
-            )
+        def load_w1(a, pieces):
+            rows = w1[a * 512 : (a + 1) * 512, :].rearrange("(p j) c -> p j c", j=PACK)
+            for lo in range(0, PACK, PACK // pieces):
+                nc.sync.dma_start(w1_raw[a][:, lo : lo + PACK // pieces, :], rows[:, lo : lo + PACK // pieces, :])
 
         gain_sb = keep.tile([P, PACK], F32, name="gain_sb")
         shift_sb = keep.tile([P, PACK], F32, name="shift_sb")
         base_sb = keep.tile([P, N_TILES], F32, name="base_sb")
-        load_w1(0)
-        nc.sync.dma_start(gain_sb[:], gain.rearrange("(p t) -> p t", t=PACK))
-        nc.sync.dma_start(list2[:], offs2)
-        nc.sync.dma_start(list3[:], offs3)
-        nc.sync.dma_start(list4[:], offs4)
-        load_w1(1)
-        load_tab(0)
+        load_w1(0, 1)
+        load_w1(1, 2)
+        load_tab(0, 4)
         nc.sync.dma_start(w2_raw[:].bitcast(I32), w2_words.rearrange("a p c -> p a c").bitcast(I32))
-        nc.sync.dma_start(shift_sb[:], shift.rearrange("(p t) -> p t", t=PACK))
+        nc.sync.dma_start(gain_sb[:], gain.rearrange("(p t) -> p t", t=PACK))
 
         picked_sc = keep.tile([P, S], U8, name="picked_sc")
         nc.vector.tensor_copy(picked_sc[:], tab_sc[:].indirect(list1[:]))
@@ -102,12 +100,12 @@ def tile_list_larval_ration_page_kernel(
         nc.vector.tensor_copy(compact[:, :S].bitcast(I32), picked_sc[:].bitcast(I32))
         planes = keep.tile([P, PASSES, S + H], U8, name="planes", align_bytes=64)
         nc.gpsimd.memset(planes[:].bitcast(I32), 0)
-        for q in range(4):
+        for q in (0, 2, 1, 3):
             nc.sync.dma_start(
                 planes[32 * q : 32 * q + 4, :, :].bitcast(I32),
                 compact[8 * q : 8 * q + 8, :].bitcast(I32),
             )
-        load_tab(1)
+        load_tab(1, 1)
 
         wgs_rows = wgs.rearrange("(q t) j -> t q j", t=PACK)
         page_rows = page0.rearrange("(p t) c -> t p c", t=PACK)
@@ -118,6 +116,11 @@ def tile_list_larval_ration_page_kernel(
             page_t = keep.tile([P, T2], F32, name="page%d" % t)
             page.append(page_t)
             nc.sync.dma_start(page_t[:], page_rows[t])
+            if t == 0:
+                nc.sync.dma_start(list2[:], offs2)
+            if t == 1:
+                nc.sync.dma_start(list3[:], offs3)
+                nc.sync.dma_start(shift_sb[:], shift.rearrange("(p t) -> p t", t=PACK))
             for lo, hi in spans:
                 dealt = keep.tile(
                     [P, hi - lo], F32, name="wgs%d_%d" % (t, lo), tag="wgs%d_%d" % (t, lo), align_bytes=64
@@ -130,6 +133,7 @@ def tile_list_larval_ration_page_kernel(
         nc.sync.dma_start(w3_raw[:], w3.rearrange("(p j) n -> p j n", j=PACK))
         wgo_sb = keep.tile([P, PICKS], F32, name="wgo_sb")
         nc.sync.dma_start(wgo_sb[:], wgo)
+        nc.sync.dma_start(list4[:], offs4)
         with nc.allow_non_contiguous_dma(reason="one bias value a partition"):
             nc.sync.dma_start(base_sb[:], base.rearrange("(c p) -> p c", p=P))
 
@@ -199,10 +203,10 @@ def tile_list_larval_ration_page_kernel(
             )
             return table, first, second
 
-        def mx_pass(acc, stationary, moving, a):
+        def mx_pass(acc, stationary, moving, start, stop):
             nc.tensor.matmul_mx(
                 out=acc, lhsT=stationary[0], lhsT_scale=stationary[1], rhs=moving[0], rhs_scale=moving[1],
-                start=(a == 0), stop=(a == PASSES - 1),
+                start=start, stop=stop,
             )
 
         def first_products(k):
@@ -213,20 +217,23 @@ def tile_list_larval_ration_page_kernel(
             if k < DIRECT:
                 for a in range(PASSES):
                     table, first, second = operands(a, t, h0, h0 + HALF)
-                    mx_pass(acc_a[:], first, table, a)
-                    mx_pass(acc_b[:], second, table, a)
+                    mx_pass(acc_a[:], first, table, a == 0, a == PASSES - 1)
+                    mx_pass(acc_b[:], second, table, a == 0, a == PASSES - 1)
                 nc.scalar.activation(tanh_a[:], acc_a[:], ACT.Tanh)
-                gated = keep.tile([P, HALF], F32, name="gated_direct")
+                gated = keep.tile([P, HALF], F32, name="gated_direct", tag="state-1", align_bytes=64)
                 nc.vector.scalar_tensor_tensor(
                     gated[:], acc_b[:], gain_sb[:, t : t + 1], tanh_a[:], ALU.mult, ALU.mult
                 )
                 sums_a[k], gated_b[k] = acc_a, gated
                 return
-            for which, acc in ((1, acc_a), (2, acc_b)):
-                for lo in range(0, HALF, P):
-                    for a in range(PASSES):
+            for a in range(PASSES):
+                for which, acc in ((1, acc_a), (2, acc_b)):
+                    for lo in range(0, HALF, P):
                         three = operands(a, t, h0 + lo, h0 + lo + P)
-                        mx_pass(acc[:, lo : lo + P], three[0], three[which], a)
+                        mx_pass(
+                            acc[:, lo : lo + P], three[0], three[which],
+                            a == 0 and lo == 0, a == PASSES - 1 and lo == HALF - P,
+                        )
             nc.scalar.activation(tanh_a[:], acc_a[:], ACT.Tanh)
             plain = ring.tile([P, HALF], F32, name="plain", bufs=3)
             nc.scalar.copy(plain[:], acc_a[:])

from contextlib import ExitStack

import concourse.mybir as mybir
from concourse.masks import make_identity

K, H, N, T, S, PICKS, T2 = 1024, 512, 384, 4096, 1024, 1024, 2048

F32 = mybir.dt.float32
BF16 = mybir.dt.bfloat16
I32 = mybir.dt.int32
U32 = mybir.dt.uint32
U16 = mybir.dt.uint16
U8 = mybir.dt.uint8
FP8X4 = mybir.dt.float8_e4m3fn_x4
FP4X4 = mybir.dt.float4_e2m1fn_x4
ACT = mybir.ActivationFunctionType
ALU = mybir.AluOpType

P = 128
PACK = 4
PASSES = K // (P * PACK)
HALF = 512
PER_COL = 16
N_TILES = N // P
DIRECT = 1
CHUNKS = ((0, 256), (256, 512), (512, 1024))

FLOPS = 2 * K * H * S * 2 + 2 * H * N * PICKS


def tile_list_larval_ration_page_kernel(
    tc, tab_words, tab_scales, offs, offs2, offs3, offs4, w1, w2_words, w2_scales,
    gain, page0, wgs, shift, w3, base, page1, wgo, out,
):
    nc = tc.nc

    def entries(offsets, lo, hi):
        return offsets[:, lo // PER_COL : hi // PER_COL]

    with ExitStack() as ctx:
        lists = ctx.enter_context(tc.tile_pool(name="lists", bufs=1))
        keep = ctx.enter_context(tc.tile_pool(name="keep", bufs=1))
        ring = ctx.enter_context(tc.tile_pool(name="ring", bufs=2))
        psum = ctx.enter_context(tc.psum_pool(name="psum", bufs=2))

        list1 = lists.tile([P, S // PER_COL], U16, name="list1")
        list2 = lists.tile([P, S // PER_COL], U16, name="list2")
        list3 = lists.tile([P, PICKS // PER_COL], U16, name="list3")
        list4 = lists.tile([P, PICKS // PER_COL], U16, name="list4")

        nc.sync.dma_start(list1[:], offs)
        tab_sc = keep.tile([P, T], U8, name="tab_sc", tag="tab_sc", align_bytes=64)
        nc.sync.dma_start(
            tab_sc[0:32, :].bitcast(I32), tab_scales.rearrange("a q t -> q a t").bitcast(I32)
        )
        nc.gpsimd.memset(tab_sc[32:64, :].bitcast(I32), 0)
        nc.vector.memset(tab_sc[64:128, :].bitcast(I32), 0)

        tab = [
            keep.tile([P, T], I32, name="tab%d" % a, tag="tab%d" % a, align_bytes=64) for a in range(PASSES)
        ]
        w1_raw = [
            keep.tile([P, PACK, H], F32, name="w1_raw%d" % a, tag="w1_raw%d" % a, align_bytes=64)
            for a in range(PASSES)
        ]
        w2_raw = keep.tile([P, PASSES, 2 * H], U8, name="w2_raw")

        def load_tab(a, pieces):
            words = tab_words[a].rearrange("p t i -> p (t i)").bitcast(I32)
            for lo in range(0, T, T // pieces):
                nc.sync.dma_start(tab[a][:, lo : lo + T // pieces], words[:, lo : lo + T // pieces])

        w2s_raw = keep.tile([P, H], U8, name="w2s_raw")
        nc.sync.dma_start(
            w2s_raw[0:32, :].bitcast(I32), w2_scales.rearrange("a q c -> q a c").bitcast(I32)
        )
        nc.gpsimd.memset(w2s_raw[32:64, :].bitcast(I32), 0)
        nc.gpsimd.memset(w2s_raw[64:128, :].bitcast(I32), 0)
        def load_w1(a, pieces):
            rows = w1[a * 512 : (a + 1) * 512, :].rearrange("(p j) c -> p j c", j=PACK)
            for lo in range(0, PACK, PACK // pieces):
                nc.sync.dma_start(w1_raw[a][:, lo : lo + PACK // pieces, :], rows[:, lo : lo + PACK // pieces, :])

        gain_sb = keep.tile([P, PACK], F32, name="gain_sb")
        shift_sb = keep.tile([P, PACK], F32, name="shift_sb")
        base_sb = keep.tile([P, N_TILES], F32, name="base_sb")
        load_w1(0, 1)
        load_w1(1, 2)
        load_tab(0, 4)
        nc.sync.dma_start(w2_raw[:].bitcast(I32), w2_words.rearrange("a p c -> p a c").bitcast(I32))
        nc.sync.dma_start(gain_sb[:], gain.rearrange("(p t) -> p t", t=PACK))

        picked_sc = keep.tile([P, S], U8, name="picked_sc")
        nc.vector.tensor_copy(picked_sc[:], tab_sc[:].indirect(list1[:]))
        compact = keep.tile([P, S + H], U8, name="compact")
        nc.vector.tensor_copy(
            compact[:, S:].rearrange("p (t q) -> p q t", t=PACK),
            w2s_raw[:].rearrange("p (q t) -> p q t", t=PACK),
        )
        nc.vector.tensor_copy(compact[:, :S].bitcast(I32), picked_sc[:].bitcast(I32))
        planes = keep.tile([P, PASSES, S + H], U8, name="planes", align_bytes=64)
        nc.gpsimd.memset(planes[:].bitcast(I32), 0)
        for q in (0, 2, 1, 3):
            nc.sync.dma_start(
                planes[32 * q : 32 * q + 4, :, :].bitcast(I32),
                compact[8 * q : 8 * q + 8, :].bitcast(I32),
            )
        load_tab(1, 1)

        wgs_rows = wgs.rearrange("(q t) j -> t q j", t=PACK)
        page_rows = page0.rearrange("(p t) c -> t p c", t=PACK)
        wgs_sb = {}
        page = []
        for t in range(PACK):
            spans = ((0, HALF), (HALF, S)) if t == 0 else ((0, S),)
            page_t = keep.tile([P, T2], F32, name="page%d" % t)
            page.append(page_t)
            nc.sync.dma_start(page_t[:], page_rows[t])
            if t == 0:
                nc.sync.dma_start(list2[:], offs2)
            if t == 1:
                nc.sync.dma_start(list3[:], offs3)
                nc.sync.dma_start(shift_sb[:], shift.rearrange("(p t) -> p t", t=PACK))
            for lo, hi in spans:
                dealt = keep.tile(
                    [P, hi - lo], F32, name="wgs%d_%d" % (t, lo), tag="wgs%d_%d" % (t, lo), align_bytes=64
                )
                for q in (0, 2, 1, 3):
                    nc.sync.dma_start(dealt[32 * q : 32 * q + 32, :], wgs_rows[t][:, lo:hi])
                for h0 in range(lo, hi, HALF):
                    wgs_sb[(t, h0)] = dealt[:, h0 - lo : h0 - lo + HALF]
        w3_raw = keep.tile([P, PACK, N], F32, name="w3_raw")
        nc.sync.dma_start(w3_raw[:], w3.rearrange("(p j) n -> p j n", j=PACK))
        wgo_sb = keep.tile([P, PICKS], F32, name="wgo_sb")
        nc.sync.dma_start(wgo_sb[:], wgo)
        nc.sync.dma_start(list4[:], offs4)
        with nc.allow_non_contiguous_dma(reason="one bias value a partition"):
            nc.sync.dma_start(base_sb[:], base.rearrange("(c p) -> p c", p=P))

        v_words = {}

        def pick_words(a):
            for h0 in range(0, S, HALF):
                words = keep.tile([P, HALF], U32, name="v_words%d_%d" % (a, h0), align_bytes=64)
                nc.vector.tensor_copy(
                    words[:], tab[a][:].bitcast(U32).indirect(entries(list1, h0, h0 + HALF))
                )
                v_words[(a, h0)] = words

        w1_codes, w1_scales = [], []
        for a in range(PASSES):
            grouped = keep.tile([P, PACK, P, PACK], BF16, name="w1_grouped%d" % a, align_bytes=64)
            nc.scalar.copy(
                grouped[:].rearrange("p t q j -> p q t j"),
                w1_raw[a][:].rearrange("p j (q t) -> p q t j", t=PACK),
            )
            codes = keep.tile([P, H], U32, name="w1_codes%d" % a, align_bytes=64)
            scales = keep.tile([P, H], U8, name="w1_scales%d" % a, align_bytes=64)
            nc.vector.quantize_mx(
                out=codes[:].bitcast(FP8X4),
                scales=scales[:],
                in_=grouped[:].rearrange("p t q j -> p (t q j)"),
            )
            w1_codes.append(codes)
            w1_scales.append(scales)

        pick_words(0)

        w2_codes = keep.tile([P, PASSES, 2 * H], U8, name="w2_codes", tag="tab0", align_bytes=64)
        nc.vector.tensor_copy(
            w2_codes[:].bitcast(U16).rearrange("p a (t q) -> p a q t", t=PACK),
            w2_raw[:].bitcast(U16).rearrange("p a (q t) -> p a q t", t=PACK),
        )

        pick_words(1)

        x_rows = [
            keep.tile([P, PACK, hi - lo], BF16, name="x_rows%d" % c) for c, (lo, hi) in enumerate(CHUNKS)
        ]

        def fetch(t, lo, hi, dst):
            nc.vector.tensor_copy(dst, page[t][:].indirect(entries(list3, lo, hi)))
            for c, (c_lo, c_hi) in enumerate(CHUNKS):
                if lo <= c_lo and c_hi <= hi:
                    nc.scalar.activation(
                        x_rows[c][:, t, :], dst[:, c_lo - lo : c_hi - lo], ACT.Identity,
                        bias=shift_sb[:, t : t + 1],
                    )

        steps = [(t, h0) for t in range(PACK) for h0 in range(0, S, HALF)]
        sums_a, gated_b, states = {}, {}, {}

        identity = keep.tile([P, P], F32, name="identity")
        make_identity(nc, identity[:])

        def operands(a, t, lo, hi):
            h0 = lo // HALF * HALF
            table = (v_words[(a, h0)][:, lo - h0 : hi - h0].bitcast(FP8X4), planes[:, a, lo:hi])
            first = (w1_codes[a][:, t * P : (t + 1) * P].bitcast(FP8X4), w1_scales[a][:, t * P : (t + 1) * P])
            second = (
                w2_codes[:, a, 2 * t * P : 2 * (t + 1) * P].bitcast(FP4X4),
                planes[:, a, S + t * P : S + (t + 1) * P],
            )
            return table, first, second

        def mx_pass(acc, stationary, moving, start, stop):
            nc.tensor.matmul_mx(
                out=acc, lhsT=stationary[0], lhsT_scale=stationary[1], rhs=moving[0], rhs_scale=moving[1],
                start=start, stop=stop,
            )

        def first_products(k):
            t, h0 = steps[k]
            acc_a = psum.tile([P, HALF], F32, name="acc_a")
            acc_b = psum.tile([P, HALF], F32, name="acc_b")
            tanh_a = ring.tile([P, HALF], F32, name="tanh_a", bufs=3)
            if k < DIRECT:
                for a in range(PASSES):
                    table, first, second = operands(a, t, h0, h0 + HALF)
                    mx_pass(acc_a[:], first, table, a == 0, a == PASSES - 1)
                    mx_pass(acc_b[:], second, table, a == 0, a == PASSES - 1)
                nc.scalar.activation(tanh_a[:], acc_a[:], ACT.Tanh)
                gated = keep.tile([P, HALF], F32, name="gated_direct", tag="state-1", align_bytes=64)
                nc.vector.scalar_tensor_tensor(
                    gated[:], acc_b[:], gain_sb[:, t : t + 1], tanh_a[:], ALU.mult, ALU.mult
                )
                sums_a[k], gated_b[k] = acc_a, gated
                return
            for a in range(PASSES):
                for which, acc in ((1, acc_a), (2, acc_b)):
                    for lo in range(0, HALF, P):
                        three = operands(a, t, h0 + lo, h0 + lo + P)
                        mx_pass(
                            acc[:, lo : lo + P], three[0], three[which],
                            a == 0 and lo == 0, a == PASSES - 1 and lo == HALF - P,
                        )
            nc.scalar.activation(tanh_a[:], acc_a[:], ACT.Tanh)
            plain = ring.tile([P, HALF], F32, name="plain", bufs=3)
            nc.scalar.copy(plain[:], acc_a[:])
            gated = keep.tile([P, HALF], F32, name="gated%d" % k, tag="state%d" % (k - 2), align_bytes=64)
            nc.vector.tensor_tensor(gated[:], acc_b[:], tanh_a[:], ALU.mult)
            sums_a[k], gated_b[k] = plain, gated

        def new_state(k):
            t = steps[k][0]
            state = keep.tile([P, HALF], F32, name="state%d" % k, tag="state%d" % k, align_bytes=64)
            if k < DIRECT:
                nc.vector.scalar_tensor_tensor(
                    state[:], sums_a[k][:], gain_sb[:, t : t + 1], gated_b[k][:], ALU.mult, ALU.add
                )
            else:
                summed = psum.tile([P, HALF], F32, name="summed")
                for lo in range(0, HALF, P):
                    for term, addend in enumerate((sums_a[k], gated_b[k])):
                        nc.tensor.matmul(
                            summed[:, lo : lo + P], addend[:, lo : lo + P], identity[:],
                            start=(term == 0), stop=(term == 1), is_transpose=True,
                        )
                nc.scalar.activation(state[:], summed[:], ACT.Copy, scale=gain_sb[:, t : t + 1])
            states[k] = state

        def put_state(k):
            t, h0 = steps[k]
            nc.vector.tensor_tensor(
                page[t][:].indirect(entries(list2, h0, h0 + HALF)), states[k][:], wgs_sb[(t, h0)], ALU.mult
            )

        first_products(0)
        for k, (t, h0) in enumerate(steps):
            if k < DIRECT:
                new_state(k)
            if k + 1 < len(steps):
                first_products(k + 1)
            if k >= DIRECT:
                new_state(k)
            if h0 == HALF and t > 0:
                early = ring.tile([P, HALF], F32, name="early")
                fetch(t - 1, 0, HALF, early[:])
            put_state(k)

        ration = []
        for n, tag in enumerate(("w1_raw0", "w1_raw1", "tab1")):
            tile_n = keep.tile([P, T2], F32, name="ration%d" % n, tag=tag, align_bytes=64)
            nc.sync.dma_start(tile_n[:], page1[n * P : (n + 1) * P, :])
            ration.append(tile_n)

        w3_grouped = keep.tile([P, N, PACK], BF16, name="w3_grouped", tag="wgs1_0", align_bytes=64)
        nc.scalar.copy(
            w3_grouped[:].rearrange("p (c i) j -> p c j i", i=4),
            w3_raw[:].rearrange("p j (c i) -> p c j i", i=4),
        )
        w3_codes = keep.tile([P, N], U32, name="w3_codes", align_bytes=64)
        w3_scales = keep.tile([P, N], U8, name="w3_scales", align_bytes=64)
        for lo, hi in ((0, 256), (256, 384)):
            nc.vector.quantize_mx(
                out=w3_codes[:, lo:hi].bitcast(FP8X4),
                scales=w3_scales[:, lo:hi],
                in_=w3_grouped[:, lo:hi, :].rearrange("p n j -> p (n j)"),
            )

        x_grouped = {}

        def weave(c):
            lo, hi = CHUNKS[c]
            grouped = keep.tile(
                [P, hi - lo, PACK], BF16, name="x_grouped%d" % c, tag="x_grouped%d" % c, align_bytes=64
            )
            nc.scalar.copy(
                grouped[:].rearrange("p (m i) t -> p m t i", i=4),
                x_rows[c][:].rearrange("p t (m i) -> p m t i", i=4),
            )
            x_grouped[c] = grouped

        features = {}

        def second_product(c):
            lo, hi = CHUNKS[c]
            codes = keep.tile([P, hi - lo], U32, name="x_codes%d" % c, align_bytes=64)
            scales = keep.tile([P, hi - lo], U8, name="x_scales%d" % c, align_bytes=64)
            nc.vector.quantize_mx(
                out=codes[:].bitcast(FP8X4), scales=scales[:],
                in_=x_grouped[c][:].rearrange("p m t -> p (m t)"),
            )
            for n in range(N_TILES):
                acc_e = psum.tile([P, HALF], F32, name="acc_e")
                nc.tensor.matmul_mx(
                    out=acc_e[:, : hi - lo],
                    lhsT=w3_codes[:, n * P : (n + 1) * P].bitcast(FP8X4),
                    lhsT_scale=w3_scales[:, n * P : (n + 1) * P],
                    rhs=codes[:].bitcast(FP8X4), rhs_scale=scales[:], start=True, stop=True,
                )
                squared = ring.tile([P, hi - lo], F32, name="squared")
                nc.scalar.activation(squared[:], acc_e[:, : hi - lo], ACT.Square)
                feature = keep.tile([P, hi - lo], F32, name="feature%d_%d" % (c, n))
                nc.scalar.activation(feature[:], squared[:], ACT.Identity, bias=base_sb[:, n : n + 1])
                features[(c, n)] = feature

        def place(c, n):
            lo, hi = CHUNKS[c]
            nc.vector.tensor_tensor(
                ration[n][:].indirect(entries(list4, lo, hi)), features[(c, n)][:], wgo_sb[:, lo:hi], ALU.mult
            )

        for c in (0, 1):
            lo, hi = CHUNKS[c]
            last = ring.tile([P, hi - lo], F32, name="last")
            fetch(PACK - 1, lo, hi, last[:])
            weave(c)
        lo, hi = CHUNKS[2]
        for t, tag in ((0, "state7"), (1, "wgs3_0")):
            held = keep.tile([P, HALF], F32, name="held%d" % t, tag=tag, align_bytes=64)
            fetch(t, lo, hi, held[:])
        second_product(0)
        late = keep.tile([P, 2, HALF], F32, name="late", tag="x_grouped0", align_bytes=64)
        for t in (2, 3):
            fetch(t, lo, hi, late[:, t - 2, :])
        second_product(1)
        weave(2)
        for n in range(N_TILES):
            place(0, n)
        second_product(2)
        for n in range(N_TILES):
            place(1, n)
        for n in range(N_TILES):
            place(2, n)
            nc.sync.dma_start(out[n * P : (n + 1) * P, :], ration[n][:])
